import numpy as np
import ml_dtypes


def mxq(x, axis, fmt="e4m3"):
    dtype, down = {"e4m3": (ml_dtypes.float8_e4m3fn, 7), "e5m2": (ml_dtypes.float8_e5m2, 14)}[fmt]
    v = np.moveaxis(np.asarray(x, np.float32).astype(ml_dtypes.bfloat16).astype(np.float64), axis, -1)
    blocks = v.reshape(v.shape[:-1] + (-1, 32))
    amax = np.abs(blocks).max(-1, keepdims=True)
    byte = np.maximum(np.where(amax > 0, np.frexp(amax)[1] - 1 + 127, 0) - down, 1)
    scale = np.exp2(byte - 127.0)
    codes = (blocks / scale).astype(np.float32).astype(dtype).astype(np.float64)
    return np.moveaxis((codes * scale).reshape(v.shape), -1, axis)


WIDE = False


def mx_kscale(k):
    if not WIDE:
        return np.ones(k)
    levels = np.array([10, -10, 5, -5, 0])
    if k % 512:
        return np.exp2(np.random.permutation(np.resize(levels, k // 32))).repeat(32)
    a = np.empty((k // 512, 16))
    for p in range(k // 512):
        a[p, :8] = np.random.permutation(np.resize(levels, 8))
        for g in range(8):
            far = levels[np.abs(levels - a[p, g]) >= 10]
            a[p, g + 8] = far[np.random.randint(len(far))]
    return np.exp2(a.ravel()).repeat(32)


def f64(x):
    return np.asarray(x).astype(np.float64)


def striped(idx):
    return np.tile(idx.reshape(-1, 16).T, (8, 1)).astype(np.uint16)


def unstriped(offs):
    return offs[:16].T.reshape(-1).astype(np.int64)


E2M1 = np.array([0.0, 0.5, 1.0, 1.5, 2.0, 3.0, 4.0, 6.0, -0.0, -0.5, -1.0, -1.5, -2.0, -3.0, -4.0, -6.0])


def pack_weight(w, fmt):
    k, n = w.shape
    w = f64(np.asarray(w, np.float32).astype(ml_dtypes.bfloat16)).reshape(k // 32, 32, n)
    amax = np.abs(w).max(1)
    if fmt == "e4m3":
        byte = np.frexp(amax)[1] - 1 + 127 - 7
    else:
        mant, ex = np.frexp(amax / 6.0)
        byte = np.where(mant > 0.5, ex, ex - 1) + 127
    byte = np.clip(np.where(amax > 0, byte, 1), 1, 254)
    scaled = (w * np.exp2(127.0 - byte)[:, None, :]).reshape(k, n).astype(np.float32)
    by_word = np.ascontiguousarray(scaled.reshape(k // 512, 128, 4, n).transpose(0, 1, 3, 2))
    if fmt == "e4m3":
        words = by_word.astype(ml_dtypes.float8_e4m3fn).view(np.uint8)
    else:
        c = by_word.astype(ml_dtypes.float4_e2m1fn).view(np.uint8) & 0xF
        words = (c[..., 0::2] | (c[..., 1::2] << 4)).reshape(k // 512, 128, 2 * n)
    return np.ascontiguousarray(words), np.ascontiguousarray(byte.astype(np.uint8).reshape(k // 512, 16, n))


def unpack_weight(words, scales, fmt):
    g, _, n = scales.shape
    words = np.ascontiguousarray(words).reshape(g, 128, n, -1)
    if fmt == "e4m3":
        vals = words.view(ml_dtypes.float8_e4m3fn).astype(np.float64)
    else:
        nib = np.empty((g, 128, n, 4), np.uint8)
        nib[..., 0::2] = words & 0xF
        nib[..., 1::2] = words >> 4
        vals = E2M1[nib]
    vals = vals * np.repeat(np.exp2(scales.astype(np.float64) - 127.0), 8, axis=1)[..., None]
    return vals.transpose(0, 1, 3, 2).reshape(g * 512, n)


def gelu(v):
    return 0.5 * v * (1.0 + np.tanh(np.sqrt(2.0 / np.pi) * (v + 0.044715 * v**3)))


def bf(x):
    return np.asarray(x, np.float32).astype(ml_dtypes.bfloat16)


def planes(Y):
    n, m = Y.shape
    b = f64(bf(Y)).reshape(n // 32, 32, m)
    amax = np.abs(b).max(1)
    byte = np.clip(np.where(amax > 0, np.frexp(amax)[1] - 1 + 127 - 7, 1), 1, 254)
    codes = (b * np.exp2(127.0 - byte)[:, None, :]).reshape(n, m).astype(np.float32).astype(ml_dtypes.float8_e4m3fn).view(np.uint8)
    words = codes.reshape(n // 512, 128, 4, m).transpose(0, 1, 3, 2)
    return np.ascontiguousarray(words), np.ascontiguousarray(byte.astype(np.uint8).reshape(n // 512, 16, m))


K, H, N, T, S, T2, P = 1024, 512, 512, 2048, 1024, 2048, 1024


def setup_inputs():
    n = np.random.standard_normal
    s = mx_kscale(K)[:, None]
    u = mx_kscale(H)[:, None]
    tab_words, tab_scales = pack_weight(n((K, T)) * s, "e4m3")
    w2_words, w2_scales = pack_weight(n((K, H)) / np.sqrt(K) / s * u.T, "e2m1")
    w5_words, w5_scales = pack_weight(2.0 * n((H, N)) / np.sqrt(H) / u, "e4m3")
    size = np.exp(0.8 * n(N))[None, :]
    return {
        "tab_words": tab_words, "tab_scales": tab_scales,
        "offs": striped(np.random.permutation(T)[:S]),
        "offs2": striped(np.random.permutation(T2)[:S]),
        "offs3": striped(np.random.permutation(T2)[:P]),
        "w1": (n((K, H)) / np.sqrt(K) / s * u.T).astype(np.float32),
        "w2_words": w2_words, "w2_scales": w2_scales,
        "w3": (1.5 * n((K, H)) / np.sqrt(K) / s).astype(np.float32),
        "gv": (np.random.uniform(0.6, 1.6, H) * u[:, 0]).astype(np.float32),
        "page0": (n((H, T2)) * u).astype(np.float32),
        "w4": (0.5 * n((H, N)) / np.sqrt(H) / u * size).astype(np.float32),
        "w5_words": w5_words, "w5_scales": w5_scales,
    }


def reference(tab_words, tab_scales, offs, offs2, offs3, w1, w2_words, w2_scales, w3, gv, page0, w4, w5_words, w5_scales):
    v = unpack_weight(tab_words, tab_scales, "e4m3")[:, unstriped(offs)]
    w2 = unpack_weight(w2_words, w2_scales, "e2m1")
    w5 = unpack_weight(w5_words, w5_scales, "e4m3")
    a = mxq(f64(w1), 0, "e4m3").T @ v
    b = w2.T @ v
    d = mxq(f64(w3), 0, "e4m3").T @ v
    h = np.maximum(a, b) + f64(gv)[:, None] * np.tanh(d)
    page = f64(page0).copy()
    l2 = unstriped(offs2)
    page[:, l2] = np.maximum(page[:, l2], h)
    x = mxq(page[:, unstriped(offs3)], 0, "e4m3")
    e = mxq(f64(w4), 0, "e4m3").T @ x
    f = w5.T @ x
    y = e + 1.0 / (1.0 + np.exp(-f))
    words, scales = planes(y)
    return y, words, scales

@@ -1,0 +1,239 @@
+from contextlib import ExitStack
+
+import concourse.mybir as mybir
+
+K, H, N, T, S, T2, M = 1024, 512, 512, 2048, 1024, 2048, 1024
+FLOPS = 2 * (3 * K * H * S + 2 * H * N * M)
+
+F32 = mybir.dt.float32
+BF16 = mybir.dt.bfloat16
+I32 = mybir.dt.int32
+U32 = mybir.dt.uint32
+U16 = mybir.dt.uint16
+U8 = mybir.dt.uint8
+FP8X4 = mybir.dt.float8_e4m3fn_x4
+FP4X4 = mybir.dt.float4_e2m1fn_x4
+ALU = mybir.AluOpType
+ACT = mybir.ActivationFunctionType
+
+P = 128
+PACK = 4
+PASS = P * PACK
+HALF = 512
+CHUNKS = [256, 256, 256, 256]
+
+
+def tile_list_sighting_credibility_page_kernel(
+    tc, tab_words, tab_scales, offs, offs2, offs3, w1, w2_words, w2_scales, w3, gv, page0, w4,
+    w5_words, w5_scales, out_0, out_1, out_2,
+):
+    nc = tc.nc
+    with ExitStack() as ctx:
+        lists = ctx.enter_context(tc.tile_pool(name="lists", bufs=1))
+        keep = ctx.enter_context(tc.tile_pool(name="keep", bufs=1))
+        work = ctx.enter_context(tc.tile_pool(name="work", bufs=2))
+        reuse = ctx.enter_context(tc.tile_pool(name="reuse", bufs=1))
+        psum = ctx.enter_context(tc.psum_pool(name="psum", bufs=8))
+
+        def kept(shape, dtype, name):
+            return keep.tile(shape, dtype, name=name, align_bytes=64)
+
+        def placed(shape, dtype, name, offset):
+            return reuse.tile(shape, dtype, name=name, align_bytes=64, offset=offset)
+
+        def bank(shape):
+            return psum.tile(shape, F32, name="bank")
+
+        idx = lists.tile([P, S // 16], U16, name="idx")
+        idx2 = lists.tile([P, S // 16], U16, name="idx2")
+        idx3 = lists.tile([P, M // 16], U16, name="idx3")
+
+        tab_plane = placed([P, T], U8, "tab_plane", 1024 * 59)
+        v_plane1 = kept([P, S], U8, "v_plane1")
+        w2_plane_in = kept([P, 2, H], U8, "w2_plane_in")
+        nc.gpsimd.memset(tab_plane[:, : T // 2].bitcast(I32), 0)
+        nc.vector.memset(tab_plane[:, T // 2 :].bitcast(I32), 0)
+        nc.gpsimd.memset(w2_plane_in[:].bitcast(I32), 0)
+        gv_sb = kept([P, PACK], F32, "gv_sb")
+        nc.gpsimd.memset(v_plane1[:].bitcast(I32), 0)
+
+        tab = [kept([P, T], I32, "tab%d" % a) for a in range(2)]
+        raw = {}
+
+        def load_tab(a):
+            nc.sync.dma_start(out=tab[a][:], in_=tab_words[a].rearrange("p t i -> p (t i)").bitcast(I32))
+
+        def load_weight(name, w, a, tile):
+            raw[name, a] = tile
+            nc.sync.dma_start(out=raw[name, a][:],
+                              in_=w[a * PASS : (a + 1) * PASS, :].rearrange("(p j) c -> p j c", j=PACK))
+
+        w2_in = kept([P, 2, 2 * H], U8, "w2_in")
+        page = [placed([P, T2], F32, "page%d" % t, 1024 * (60, 32, 44, 52)[t]) for t in range(PACK)]
+        page_rows = page0.rearrange("(p t) c -> p t c", t=PACK)
+
+        nc.sync.dma_start(idx[:], offs)
+        nc.sync.dma_start(idx2[:], offs2)
+        nc.sync.dma_start(idx3[:], offs3)
+        load_tab(0)
+        nc.sync.dma_start(out=gv_sb[:], in_=gv.rearrange("(p t) -> p t", t=PACK))
+        nc.sync.dma_start(out=w2_in[:].bitcast(I32), in_=w2_words.rearrange("a p c -> p a c").bitcast(I32))
+        for q in range(4):
+            nc.sync.dma_start(out=tab_plane[32 * q : 32 * q + 8, :].bitcast(I32),
+                              in_=tab_scales[:, 4 * q : 4 * q + 4, :].bitcast(I32))
+        load_tab(1)
+        load_weight("w1", w1, 0, kept([P, PACK, H], F32, "raw_w1_0"))
+        for q in range(4):
+            nc.sync.dma_start(out=w2_plane_in[32 * q : 32 * q + 4, :, :].bitcast(I32),
+                              in_=w2_scales[:, 4 * q : 4 * q + 4, :].rearrange("a r c -> r a c").bitcast(I32))
+        load_weight("w1", w1, 1, placed([P, PACK, H], F32, "raw_w1_1", 1024 * 32))
+        load_weight("w3", w3, 0, placed([P, PACK, H], F32, "raw_w3_0", 1024 * 40))
+
+        v_words = [kept([P, S], U32, "v_words%d" % a) for a in range(2)]
+        v_plane = kept([P, S], U8, "v_plane")
+        nc.vector.tensor_copy(v_words[0][:], tab[0][:].bitcast(U32).indirect(idx[:]))
+        nc.vector.tensor_copy(v_plane[:], tab_plane[:].indirect(idx[:]))
+        for q in range(4):
+            nc.sync.dma_start(out=v_plane1[32 * q : 32 * q + 4, :].bitcast(I32),
+                              in_=v_plane[32 * q + 4 : 32 * q + 8, :].bitcast(I32))
+        load_weight("w3", w3, 1, placed([P, PACK, H], F32, "raw_w3_1", 1024 * 52))
+        nc.sync.dma_start(out=page[0][:], in_=page_rows[:, 0, :])
+        nc.vector.tensor_copy(v_words[1][:], tab[1][:].bitcast(U32).indirect(idx[:]))
+
+        codes, planes = {}, {}
+
+        def quantise_weight(name, a, copy, offset):
+            dealt = placed([P, PACK * H], BF16, "dealt_%s_%d" % (name, a), offset)
+            copy(dealt[:].rearrange("p (t m j) -> p m j t", t=PACK, j=PACK),
+                 raw[name, a][:].rearrange("p j (m t) -> p m j t", t=PACK))
+            codes[name, a] = kept([P, H], U32, "codes_%s_%d" % (name, a))
+            planes[name, a] = kept([P, H], U8, "plane_%s_%d" % (name, a))
+            nc.vector.quantize_mx(out=codes[name, a][:].bitcast(FP8X4), scales=planes[name, a][:], in_=dealt[:])
+
+        quantise_weight("w1", 0, nc.scalar.copy, 2048)
+        w2_plane = kept([P, 2, H], U8, "w2_plane")
+        nc.vector.tensor_copy(w2_plane[:].rearrange("p a (t m) -> p a t m", t=PACK),
+                              w2_plane_in[:].rearrange("p a (m t) -> p a t m", t=PACK))
+        w2_codes = kept([P, 2, 2 * H], U8, "w2_codes")
+        nc.vector.tensor_copy(w2_codes[:].bitcast(U16).rearrange("p a (t m) -> p a t m", t=PACK),
+                              w2_in[:].bitcast(U16).rearrange("p a (m t) -> p a t m", t=PACK))
+        quantise_weight("w1", 1, nc.scalar.copy, 16384)
+        quantise_weight("w3", 0, nc.scalar.copy, 2048)
+        quantise_weight("w3", 1, nc.vector.tensor_copy, 16384)
+
+        for t in range(1, PACK):
+            nc.sync.dma_start(out=page[t][:], in_=page_rows[:, t, :])
+
+        def first_product(out, name, t, cols):
+            rows = slice(t * P, (t + 1) * P)
+            for a in range(2):
+                if name == "w2":
+                    lhsT = w2_codes[:, a, 2 * t * P : 2 * (t + 1) * P].bitcast(FP4X4)
+                    lhsT_scale = w2_plane[:, a, rows]
+                    rhs_scale = (v_plane, v_plane1)[a][:, cols]
+                else:
+                    lhsT = codes[name, a][:, rows].bitcast(FP8X4)
+                    lhsT_scale = planes[name, a][:, rows]
+                    rhs_scale = v_plane[4 * a : P, cols]
+                nc.tensor.matmul_mx(out=out[:], lhsT=lhsT, lhsT_scale=lhsT_scale,
+                                    rhs=v_words[a][:, cols].bitcast(FP8X4), rhs_scale=rhs_scale,
+                                    start=(a == 0), stop=(a == 1))
+
+        for t in range(PACK):
+            old = placed([P, S], F32, "old%d" % t, 4096 if t == 1 else 0)
+            nc.vector.tensor_copy(old[:], page[t][:].indirect(idx2[:]))
+            for hf in range(S // HALF):
+                cols = slice(hf * HALF, (hf + 1) * HALF)
+                b_ps, a_ps, d_ps = bank([P, HALF]), bank([P, HALF]), bank([P, HALF])
+                first_product(b_ps, "w2", t, cols)
+                first_product(a_ps, "w1", t, cols)
+                first_product(d_ps, "w3", t, cols)
+                b_sb = placed([P, HALF], F32, "b_sb%d_%d" % (t, hf), 1024 * 40 + 2048 * hf)
+                nc.scalar.copy(b_sb[:], b_ps[:])
+                th = work.tile([P, HALF], F32, name="th")
+                nc.scalar.activation(th[:], d_ps[:], ACT.Tanh)
+                larger = placed([P, HALF], F32, "larger%d_%d" % (t, hf), 16384 + 2048 * hf)
+                nc.vector.tensor_tensor(larger[:], a_ps[:], b_sb[:], ALU.max)
+                h = work.tile([P, HALF], F32, name="h")
+                nc.vector.scalar_tensor_tensor(h[:], th[:], gv_sb[:, t : t + 1], larger[:], ALU.mult, ALU.add)
+                new = placed([P, HALF], F32, "new%d_%d" % (t, hf), 20480 + 2048 * hf)
+                nc.vector.tensor_tensor(new[:], h[:], old[:, cols], ALU.max)
+                nc.vector.tensor_copy(page[t][:].indirect(idx2[:, hf * HALF // 16 : (hf + 1) * HALF // 16]), new[:])
+            if t == 1:
+                w5_plane_in = placed([P, N], U8, "w5_plane_in", 4096)
+                w5_in = placed([P, N], I32, "w5_in", 4608)
+                load_weight("w4", w4, 0, placed([P, PACK, N], F32, "raw_w4", 6656))
+                nc.sync.dma_start(out=w5_in[:], in_=w5_words[0].rearrange("p c i -> p (c i)").bitcast(I32))
+                nc.vector.memset(w5_plane_in[:].bitcast(I32), 0)
+                for q in range(4):
+                    nc.sync.dma_start(out=w5_plane_in[32 * q : 32 * q + 4, :].bitcast(I32),
+                                      in_=w5_scales[0, 4 * q : 4 * q + 4, :].bitcast(I32))
+            if t == 2:
+                quantise_weight("w4", 0, nc.scalar.copy, 1024 * 24)
+                w5_codes = kept([P, N], I32, "w5_codes")
+                nc.vector.tensor_copy(w5_codes[:].rearrange("p (t m) -> p m t", t=PACK),
+                                      w5_in[:].rearrange("p (m t) -> p m t", t=PACK))
+                w5_plane = kept([P, N], U8, "w5_plane")
+                nc.vector.tensor_copy(w5_plane[:].rearrange("p (t m) -> p t m", t=PACK),
+                                      w5_plane_in[:].rearrange("p (m t) -> p t m", t=PACK))
+
+        y_codes = kept([P, M], I32, "y_codes")
+        y_plane = kept([P, M], U8, "y_plane")
+        out_rows = out_0.rearrange("(p t) m -> p t m", t=PACK)
+        out_words = out_1[0].rearrange("p m i -> p (m i)").bitcast(I32)
+        starts = [sum(CHUNKS[:c]) for c in range(len(CHUNKS))]
+        x_bf, x_codes, x_plane, e_ps, gate, y_bf = {}, {}, {}, {}, {}, {}
+
+        def look_up(c):
+            n, m0 = CHUNKS[c], starts[c]
+            picked = placed([P, PACK, n], BF16, "picked%d" % c, 69632 + 2048 if c == 3 else 20480 + 2048 * (c % 2))
+            for t in range(PACK):
+                nc.vector.tensor_copy(picked[:, t, :], page[t][:].indirect(idx3[:, m0 // 16 : (m0 + n) // 16]))
+            x_bf[c] = kept([P, PACK * n], BF16, "x_bf%d" % c)
+            nc.scalar.copy(x_bf[c][:].rearrange("p (g i t) -> p g t i", i=4, t=PACK),
+                           picked[:].rearrange("p t (g i) -> p g t i", i=4))
+
+        def quantise_x(c):
+            n = CHUNKS[c]
+            x_codes[c] = kept([P, n], U32, "x_codes%d" % c)
+            x_plane[c] = kept([P, n], U8, "x_plane%d" % c)
+            nc.vector.quantize_mx(out=x_codes[c][:].bitcast(FP8X4), scales=x_plane[c][:], in_=x_bf[c][:])
+
+        def products(c):
+            n = CHUNKS[c]
+            per_bank = HALF // n
+            for t0 in range(0, PACK, per_bank):
+                f_ps, e_ps[c, t0] = bank([P, per_bank, n]), bank([P, per_bank, n])
+                for ps, words, plane in ((f_ps, w5_codes, w5_plane), (e_ps[c, t0], codes["w4", 0], planes["w4", 0])):
+                    for i in range(per_bank):
+                        rows = slice((t0 + i) * P, (t0 + i + 1) * P)
+                        nc.tensor.matmul_mx(out=ps[:, i, :], lhsT=words[:, rows].bitcast(FP8X4),
+                                            lhsT_scale=plane[:, rows], rhs=x_codes[c][:].bitcast(FP8X4),
+                                            rhs_scale=x_plane[c][:], start=True, stop=True)
+                gate[c, t0] = placed([P, per_bank, n], F32, "gate%d_%d" % (c, t0), 69632 + 4096 * (c % 2) + 1024 * t0)
+                nc.scalar.activation(gate[c, t0][:], f_ps[:], ACT.Sigmoid)
+
+        def results(c):
+            n, m0 = CHUNKS[c], starts[c]
+            per_bank = HALF // n
+            y = kept([P, PACK, n], F32, "y%d" % c)
+            for t0 in range(0, PACK, per_bank):
+                nc.vector.tensor_tensor(y[:, t0 : t0 + per_bank, :], e_ps[c, t0][:], gate[c, t0][:], ALU.add)
+            nc.sync.dma_start(out=out_rows[:, :, m0 : m0 + n], in_=y[:])
+            y_bf[c] = kept([P, PACK * n], BF16, "y_bf%d" % c)
+            copy = nc.vector.tensor_copy if c == len(CHUNKS) - 1 else nc.scalar.copy
+            copy(y_bf[c][:].rearrange("p (g i t) -> p g t i", i=4, t=PACK),
+                 y[:].rearrange("p t (g i) -> p g t i", i=4))
+
+        def quantise_y(c):
+            cols = slice(starts[c], starts[c] + CHUNKS[c])
+            nc.vector.quantize_mx(out=y_codes[:, cols].bitcast(FP8X4), scales=y_plane[:, cols], in_=y_bf[c][:])
+            nc.sync.dma_start(out=out_words[:, cols], in_=y_codes[:, cols])
+
+        for i in range(len(CHUNKS) + 4):
+            for step, lag in ((results, 3), (look_up, 0), (quantise_x, 1), (products, 1), (quantise_y, 4)):
+                if 0 <= i - lag < len(CHUNKS):
+                    step(i - lag)
+        for q in range(4):
+            nc.sync.dma_start(out=out_2[0, 4 * q : 4 * q + 4, :].bitcast(I32),
+                              in_=y_plane[32 * q : 32 * q + 4, :].bitcast(I32))

@@ -33,7 +33,7 @@ def tile_list_sighting_credibility_page_kernel(
         keep = ctx.enter_context(tc.tile_pool(name="keep", bufs=1))
         work = ctx.enter_context(tc.tile_pool(name="work", bufs=2))
         reuse = ctx.enter_context(tc.tile_pool(name="reuse", bufs=1))
-        psum = ctx.enter_context(tc.psum_pool(name="psum", bufs=8))
+        psum = ctx.enter_context(tc.psum_pool(name="psum", bufs=1))
 
         def kept(shape, dtype, name):
             return keep.tile(shape, dtype, name=name, align_bytes=64)
@@ -41,8 +41,8 @@ def tile_list_sighting_credibility_page_kernel(
         def placed(shape, dtype, name, offset):
             return reuse.tile(shape, dtype, name=name, align_bytes=64, offset=offset)
 
-        def bank(shape):
-            return psum.tile(shape, F32, name="bank")
+        def bank(shape, name, number):
+            return psum.tile(shape, F32, name=name, offset=2048 * number)
 
         idx = lists.tile([P, S // 16], U16, name="idx")
         idx2 = lists.tile([P, S // 16], U16, name="idx2")
@@ -69,24 +69,25 @@ def tile_list_sighting_credibility_page_kernel(
                               in_=w[a * PASS : (a + 1) * PASS, :].rearrange("(p j) c -> p j c", j=PACK))
 
         w2_in = kept([P, 2, 2 * H], U8, "w2_in")
-        page = [placed([P, T2], F32, "page%d" % t, 1024 * (60, 32, 44, 52)[t]) for t in range(PACK)]
+        page = [placed([P, T2], F32, "page%d" % t, 1024 * (60, 32, 40, 48)[t]) for t in range(PACK)]
         page_rows = page0.rearrange("(p t) c -> p t c", t=PACK)
 
         nc.sync.dma_start(idx[:], offs)
         nc.sync.dma_start(idx2[:], offs2)
         nc.sync.dma_start(idx3[:], offs3)
         load_tab(0)
-        nc.sync.dma_start(out=gv_sb[:], in_=gv.rearrange("(p t) -> p t", t=PACK))
         nc.sync.dma_start(out=w2_in[:].bitcast(I32), in_=w2_words.rearrange("a p c -> p a c").bitcast(I32))
         for q in range(4):
-            nc.sync.dma_start(out=tab_plane[32 * q : 32 * q + 8, :].bitcast(I32),
-                              in_=tab_scales[:, 4 * q : 4 * q + 4, :].bitcast(I32))
+            nc.sync.dma_start(out=tab_plane[32 * q : 32 * q + 4, :].bitcast(I32),
+                              in_=tab_scales[0, 4 * q : 4 * q + 4, :].bitcast(I32))
+        nc.sync.dma_start(out=tab_plane[16:32, :].bitcast(I32), in_=tab_scales[1].bitcast(I32))
         load_tab(1)
         load_weight("w1", w1, 0, kept([P, PACK, H], F32, "raw_w1_0"))
         for q in range(4):
             nc.sync.dma_start(out=w2_plane_in[32 * q : 32 * q + 4, :, :].bitcast(I32),
                               in_=w2_scales[:, 4 * q : 4 * q + 4, :].rearrange("a r c -> r a c").bitcast(I32))
         load_weight("w1", w1, 1, placed([P, PACK, H], F32, "raw_w1_1", 1024 * 32))
+        nc.sync.dma_start(out=gv_sb[:], in_=gv.rearrange("(p t) -> p t", t=PACK))
         load_weight("w3", w3, 0, placed([P, PACK, H], F32, "raw_w3_0", 1024 * 40))
 
         v_words = [kept([P, S], U32, "v_words%d" % a) for a in range(2)]
@@ -95,31 +96,35 @@ def tile_list_sighting_credibility_page_kernel(
         nc.vector.tensor_copy(v_plane[:], tab_plane[:].indirect(idx[:]))
         for q in range(4):
             nc.sync.dma_start(out=v_plane1[32 * q : 32 * q + 4, :].bitcast(I32),
-                              in_=v_plane[32 * q + 4 : 32 * q + 8, :].bitcast(I32))
+                              in_=v_plane[16 + 4 * q : 20 + 4 * q, :].bitcast(I32))
         load_weight("w3", w3, 1, placed([P, PACK, H], F32, "raw_w3_1", 1024 * 52))
         nc.sync.dma_start(out=page[0][:], in_=page_rows[:, 0, :])
         nc.vector.tensor_copy(v_words[1][:], tab[1][:].bitcast(U32).indirect(idx[:]))
 
         codes, planes = {}, {}
 
-        def quantise_weight(name, a, copy, offset):
-            dealt = placed([P, PACK * H], BF16, "dealt_%s_%d" % (name, a), offset)
-            copy(dealt[:].rearrange("p (t m j) -> p m j t", t=PACK, j=PACK),
-                 raw[name, a][:].rearrange("p j (m t) -> p m j t", t=PACK))
+        def quantise_weight(name, a, parts):
             codes[name, a] = kept([P, H], U32, "codes_%s_%d" % (name, a))
             planes[name, a] = kept([P, H], U8, "plane_%s_%d" % (name, a))
-            nc.vector.quantize_mx(out=codes[name, a][:].bitcast(FP8X4), scales=planes[name, a][:], in_=dealt[:])
+            slices = PACK // len(parts)
+            for i, (copy, offset) in enumerate(parts):
+                dealt = placed([P, slices * PASS], BF16, "dealt_%s_%d_%d" % (name, a, i), offset)
+                copy(dealt[:].rearrange("p (t m j) -> p m j t", t=slices, j=PACK),
+                     raw[name, a][:].rearrange("p j (m t) -> p m j t", t=PACK)[:, :, :, i * slices : (i + 1) * slices])
+                cols = slice(i * slices * P, (i + 1) * slices * P)
+                nc.vector.quantize_mx(out=codes[name, a][:, cols].bitcast(FP8X4), scales=planes[name, a][:, cols],
+                                      in_=dealt[:])
 
-        quantise_weight("w1", 0, nc.scalar.copy, 2048)
+        quantise_weight("w1", 0, [(nc.scalar.copy, 0)])
         w2_plane = kept([P, 2, H], U8, "w2_plane")
         nc.vector.tensor_copy(w2_plane[:].rearrange("p a (t m) -> p a t m", t=PACK),
                               w2_plane_in[:].rearrange("p a (m t) -> p a t m", t=PACK))
         w2_codes = kept([P, 2, 2 * H], U8, "w2_codes")
         nc.vector.tensor_copy(w2_codes[:].bitcast(U16).rearrange("p a (t m) -> p a t m", t=PACK),
                               w2_in[:].bitcast(U16).rearrange("p a (m t) -> p a t m", t=PACK))
-        quantise_weight("w1", 1, nc.scalar.copy, 16384)
-        quantise_weight("w3", 0, nc.scalar.copy, 2048)
-        quantise_weight("w3", 1, nc.vector.tensor_copy, 16384)
+        quantise_weight("w1", 1, [(nc.scalar.copy, 4096)])
+        quantise_weight("w3", 0, [(nc.vector.tensor_copy, 0)])
+        quantise_weight("w3", 1, [(nc.vector.tensor_copy, 3072), (nc.scalar.copy, 17408)])
 
         for t in range(1, PACK):
             nc.sync.dma_start(out=page[t][:], in_=page_rows[:, t, :])
@@ -130,13 +135,11 @@ def tile_list_sighting_credibility_page_kernel(
                 if name == "w2":
                     lhsT = w2_codes[:, a, 2 * t * P : 2 * (t + 1) * P].bitcast(FP4X4)
                     lhsT_scale = w2_plane[:, a, rows]
-                    rhs_scale = (v_plane, v_plane1)[a][:, cols]
                 else:
                     lhsT = codes[name, a][:, rows].bitcast(FP8X4)
                     lhsT_scale = planes[name, a][:, rows]
-                    rhs_scale = v_plane[4 * a : P, cols]
                 nc.tensor.matmul_mx(out=out[:], lhsT=lhsT, lhsT_scale=lhsT_scale,
-                                    rhs=v_words[a][:, cols].bitcast(FP8X4), rhs_scale=rhs_scale,
+                                    rhs=v_words[a][:, cols].bitcast(FP8X4), rhs_scale=(v_plane, v_plane1)[a][:, cols],
                                     start=(a == 0), stop=(a == 1))
 
         for t in range(PACK):
@@ -144,18 +147,22 @@ def tile_list_sighting_credibility_page_kernel(
             nc.vector.tensor_copy(old[:], page[t][:].indirect(idx2[:]))
             for hf in range(S // HALF):
                 cols = slice(hf * HALF, (hf + 1) * HALF)
-                b_ps, a_ps, d_ps = bank([P, HALF]), bank([P, HALF]), bank([P, HALF])
+                unit = "%d_%d" % (t, hf)
+                a_ps, b_ps, d_ps = (bank([P, HALF], "a" + unit, hf), bank([P, HALF], "b" + unit, 2 + hf),
+                                    bank([P, HALF], "d" + unit, 4 + hf))
                 first_product(b_ps, "w2", t, cols)
                 first_product(a_ps, "w1", t, cols)
                 first_product(d_ps, "w3", t, cols)
-                b_sb = placed([P, HALF], F32, "b_sb%d_%d" % (t, hf), 1024 * 40 + 2048 * hf)
+                b_sb = placed([P, HALF], F32, "b_sb%d_%d" % (t, hf), 1024 * 56 + 2048 * hf)
                 nc.scalar.copy(b_sb[:], b_ps[:])
                 th = work.tile([P, HALF], F32, name="th")
                 nc.scalar.activation(th[:], d_ps[:], ACT.Tanh)
                 larger = placed([P, HALF], F32, "larger%d_%d" % (t, hf), 16384 + 2048 * hf)
                 nc.vector.tensor_tensor(larger[:], a_ps[:], b_sb[:], ALU.max)
+                bounded = work.tile([P, HALF], F32, name="bounded")
+                nc.scalar.activation(bounded[:], th[:], ACT.Copy, scale=gv_sb[:, t : t + 1])
                 h = work.tile([P, HALF], F32, name="h")
-                nc.vector.scalar_tensor_tensor(h[:], th[:], gv_sb[:, t : t + 1], larger[:], ALU.mult, ALU.add)
+                nc.gpsimd.tensor_tensor(h[:], larger[:], bounded[:], ALU.add)
                 new = placed([P, HALF], F32, "new%d_%d" % (t, hf), 20480 + 2048 * hf)
                 nc.vector.tensor_tensor(new[:], h[:], old[:, cols], ALU.max)
                 nc.vector.tensor_copy(page[t][:].indirect(idx2[:, hf * HALF // 16 : (hf + 1) * HALF // 16]), new[:])
@@ -164,17 +171,17 @@ def tile_list_sighting_credibility_page_kernel(
                 w5_in = placed([P, N], I32, "w5_in", 4608)
                 load_weight("w4", w4, 0, placed([P, PACK, N], F32, "raw_w4", 6656))
                 nc.sync.dma_start(out=w5_in[:], in_=w5_words[0].rearrange("p c i -> p (c i)").bitcast(I32))
-                nc.vector.memset(w5_plane_in[:].bitcast(I32), 0)
+                nc.gpsimd.memset(w5_plane_in[:].bitcast(I32), 0)
                 for q in range(4):
                     nc.sync.dma_start(out=w5_plane_in[32 * q : 32 * q + 4, :].bitcast(I32),
                                       in_=w5_scales[0, 4 * q : 4 * q + 4, :].bitcast(I32))
             if t == 2:
-                quantise_weight("w4", 0, nc.scalar.copy, 1024 * 24)
+                quantise_weight("w4", 0, [(nc.scalar.copy, 1024 * 24)])
                 w5_codes = kept([P, N], I32, "w5_codes")
-                nc.vector.tensor_copy(w5_codes[:].rearrange("p (t m) -> p m t", t=PACK),
+                nc.gpsimd.tensor_copy(w5_codes[:].rearrange("p (t m) -> p m t", t=PACK),
                                       w5_in[:].rearrange("p (m t) -> p m t", t=PACK))
                 w5_plane = kept([P, N], U8, "w5_plane")
-                nc.vector.tensor_copy(w5_plane[:].rearrange("p (t m) -> p t m", t=PACK),
+                nc.gpsimd.tensor_copy(w5_plane[:].rearrange("p (t m) -> p t m", t=PACK),
                                       w5_plane_in[:].rearrange("p (m t) -> p t m", t=PACK))
 
         y_codes = kept([P, M], I32, "y_codes")
@@ -203,7 +210,8 @@ def tile_list_sighting_credibility_page_kernel(
             n = CHUNKS[c]
             per_bank = HALF // n
             for t0 in range(0, PACK, per_bank):
-                f_ps, e_ps[c, t0] = bank([P, per_bank, n]), bank([P, per_bank, n])
+                f_ps = bank([P, per_bank, n], "f%d_%d" % (c, t0), 2 + 2 * (c % 2) + t0 // per_bank)
+                e_ps[c, t0] = bank([P, per_bank, n], "e%d_%d" % (c, t0), 6 * (c % 2) + t0 // per_bank)
                 for ps, words, plane in ((f_ps, w5_codes, w5_plane), (e_ps[c, t0], codes["w4", 0], planes["w4", 0])):
                     for i in range(per_bank):
                         rows = slice((t0 + i) * P, (t0 + i + 1) * P)

@@ -20,6 +20,7 @@ P = 128
 PACK = 4
 PASS = P * PACK
 HALF = 512
+KB = 1024
 CHUNKS = [256, 256, 256, 256]
 
 
@@ -48,60 +49,63 @@ def tile_list_sighting_credibility_page_kernel(
         idx2 = lists.tile([P, S // 16], U16, name="idx2")
         idx3 = lists.tile([P, M // 16], U16, name="idx3")
 
-        tab_plane = placed([P, T], U8, "tab_plane", 1024 * 59)
+        tab_plane = kept([P, T], U8, "tab_plane")
         v_plane1 = kept([P, S], U8, "v_plane1")
         w2_plane_in = kept([P, 2, H], U8, "w2_plane_in")
+        w5_plane_in = kept([P, N], U8, "w5_plane_in")
         nc.gpsimd.memset(tab_plane[:, : T // 2].bitcast(I32), 0)
         nc.vector.memset(tab_plane[:, T // 2 :].bitcast(I32), 0)
         nc.gpsimd.memset(w2_plane_in[:].bitcast(I32), 0)
-        gv_sb = kept([P, PACK], F32, "gv_sb")
         nc.gpsimd.memset(v_plane1[:].bitcast(I32), 0)
+        nc.gpsimd.memset(w5_plane_in[:].bitcast(I32), 0)
 
-        tab = [kept([P, T], I32, "tab%d" % a) for a in range(2)]
-        raw = {}
+        tab, raw, page, codes, planes, larger, old = {}, {}, {}, {}, {}, {}, {}
+        page_rows = page0.rearrange("(p t) c -> p t c", t=PACK)
+        w2_in = kept([P, 2, 2 * H], U8, "w2_in")
+        w5_in = kept([P, N], I32, "w5_in")
+        gv_sb = kept([P, PACK], F32, "gv_sb")
+        v_words = [kept([P, S], U32, "v_words%d" % a) for a in range(2)]
+        v_plane = kept([P, S], U8, "v_plane")
+        w2_codes = kept([P, 2, 2 * H], U8, "w2_codes")
+        w2_plane = kept([P, 2, H], U8, "w2_plane")
 
         def load_tab(a):
+            tab[a] = placed([P, T], I32, "tab%d" % a, 8 * a * KB)
             nc.sync.dma_start(out=tab[a][:], in_=tab_words[a].rearrange("p t i -> p (t i)").bitcast(I32))
 
-        def load_weight(name, w, a, tile):
-            raw[name, a] = tile
+        def load_tab_scales():
+            for q in range(4):
+                nc.sync.dma_start(out=tab_plane[32 * q : 32 * q + 4, :].bitcast(I32),
+                                  in_=tab_scales[0, 4 * q : 4 * q + 4, :].bitcast(I32))
+            nc.sync.dma_start(out=tab_plane[16:32, :].bitcast(I32), in_=tab_scales[1].bitcast(I32))
+
+        def load_w2_scales():
+            for q in range(4):
+                nc.sync.dma_start(out=w2_plane_in[32 * q : 32 * q + 4, :, :].bitcast(I32),
+                                  in_=w2_scales[:, 4 * q : 4 * q + 4, :].rearrange("a r c -> r a c").bitcast(I32))
+
+        def load_w5():
+            nc.sync.dma_start(out=w5_in[:], in_=w5_words[0].rearrange("p c i -> p (c i)").bitcast(I32))
+            for q in range(4):
+                nc.sync.dma_start(out=w5_plane_in[32 * q : 32 * q + 4, :].bitcast(I32),
+                                  in_=w5_scales[0, 4 * q : 4 * q + 4, :].bitcast(I32))
+
+        def load_weight(name, w, a, offset):
+            raw[name, a] = placed([P, PACK, H], F32, "raw_%s_%d" % (name, a), offset)
             nc.sync.dma_start(out=raw[name, a][:],
                               in_=w[a * PASS : (a + 1) * PASS, :].rearrange("(p j) c -> p j c", j=PACK))
 
-        w2_in = kept([P, 2, 2 * H], U8, "w2_in")
-        page = [placed([P, T2], F32, "page%d" % t, 1024 * (60, 32, 40, 48)[t]) for t in range(PACK)]
-        page_rows = page0.rearrange("(p t) c -> p t c", t=PACK)
+        def load_page(t, offset):
+            page[t] = placed([P, T2], F32, "page%d" % t, offset)
+            nc.sync.dma_start(out=page[t][:], in_=page_rows[:, t, :])
 
-        nc.sync.dma_start(idx[:], offs)
-        nc.sync.dma_start(idx2[:], offs2)
-        nc.sync.dma_start(idx3[:], offs3)
-        load_tab(0)
-        nc.sync.dma_start(out=w2_in[:].bitcast(I32), in_=w2_words.rearrange("a p c -> p a c").bitcast(I32))
-        for q in range(4):
-            nc.sync.dma_start(out=tab_plane[32 * q : 32 * q + 4, :].bitcast(I32),
-                              in_=tab_scales[0, 4 * q : 4 * q + 4, :].bitcast(I32))
-        nc.sync.dma_start(out=tab_plane[16:32, :].bitcast(I32), in_=tab_scales[1].bitcast(I32))
-        load_tab(1)
-        load_weight("w1", w1, 0, kept([P, PACK, H], F32, "raw_w1_0"))
-        for q in range(4):
-            nc.sync.dma_start(out=w2_plane_in[32 * q : 32 * q + 4, :, :].bitcast(I32),
-                              in_=w2_scales[:, 4 * q : 4 * q + 4, :].rearrange("a r c -> r a c").bitcast(I32))
-        load_weight("w1", w1, 1, placed([P, PACK, H], F32, "raw_w1_1", 1024 * 32))
-        nc.sync.dma_start(out=gv_sb[:], in_=gv.rearrange("(p t) -> p t", t=PACK))
-        load_weight("w3", w3, 0, placed([P, PACK, H], F32, "raw_w3_0", 1024 * 40))
+        def gather_words(a):
+            nc.vector.tensor_copy(v_words[a][:], tab[a][:].bitcast(U32).indirect(idx[:]))
 
-        v_words = [kept([P, S], U32, "v_words%d" % a) for a in range(2)]
-        v_plane = kept([P, S], U8, "v_plane")
-        nc.vector.tensor_copy(v_words[0][:], tab[0][:].bitcast(U32).indirect(idx[:]))
-        nc.vector.tensor_copy(v_plane[:], tab_plane[:].indirect(idx[:]))
-        for q in range(4):
-            nc.sync.dma_start(out=v_plane1[32 * q : 32 * q + 4, :].bitcast(I32),
-                              in_=v_plane[16 + 4 * q : 20 + 4 * q, :].bitcast(I32))
-        load_weight("w3", w3, 1, placed([P, PACK, H], F32, "raw_w3_1", 1024 * 52))
-        nc.sync.dma_start(out=page[0][:], in_=page_rows[:, 0, :])
-        nc.vector.tensor_copy(v_words[1][:], tab[1][:].bitcast(U32).indirect(idx[:]))
-
-        codes, planes = {}, {}
+        def move_scale_rows():
+            for q in range(4):
+                nc.sync.dma_start(out=v_plane1[32 * q : 32 * q + 4, :].bitcast(I32),
+                                  in_=v_plane[16 + 4 * q : 20 + 4 * q, :].bitcast(I32))
 
         def quantise_weight(name, a, parts):
             codes[name, a] = kept([P, H], U32, "codes_%s_%d" % (name, a))
@@ -115,19 +119,13 @@ def tile_list_sighting_credibility_page_kernel(
                 nc.vector.quantize_mx(out=codes[name, a][:, cols].bitcast(FP8X4), scales=planes[name, a][:, cols],
                                       in_=dealt[:])
 
-        quantise_weight("w1", 0, [(nc.scalar.copy, 0)])
-        w2_plane = kept([P, 2, H], U8, "w2_plane")
-        nc.vector.tensor_copy(w2_plane[:].rearrange("p a (t m) -> p a t m", t=PACK),
-                              w2_plane_in[:].rearrange("p a (m t) -> p a t m", t=PACK))
-        w2_codes = kept([P, 2, 2 * H], U8, "w2_codes")
-        nc.vector.tensor_copy(w2_codes[:].bitcast(U16).rearrange("p a (t m) -> p a t m", t=PACK),
-                              w2_in[:].bitcast(U16).rearrange("p a (m t) -> p a t m", t=PACK))
-        quantise_weight("w1", 1, [(nc.scalar.copy, 4096)])
-        quantise_weight("w3", 0, [(nc.vector.tensor_copy, 0)])
-        quantise_weight("w3", 1, [(nc.vector.tensor_copy, 3072), (nc.scalar.copy, 17408)])
+        def deal_w2_words():
+            nc.vector.tensor_copy(w2_codes[:].bitcast(U16).rearrange("p a (t m) -> p a t m", t=PACK),
+                                  w2_in[:].bitcast(U16).rearrange("p a (m t) -> p a t m", t=PACK))
 
-        for t in range(1, PACK):
-            nc.sync.dma_start(out=page[t][:], in_=page_rows[:, t, :])
+        def deal_w2_scales():
+            nc.vector.tensor_copy(w2_plane[:].rearrange("p a (t m) -> p a t m", t=PACK),
+                                  w2_plane_in[:].rearrange("p a (m t) -> p a t m", t=PACK))
 
         def first_product(out, name, t, cols):
             rows = slice(t * P, (t + 1) * P)
@@ -139,44 +137,79 @@ def tile_list_sighting_credibility_page_kernel(
                     lhsT = codes[name, a][:, rows].bitcast(FP8X4)
                     lhsT_scale = planes[name, a][:, rows]
                 nc.tensor.matmul_mx(out=out[:], lhsT=lhsT, lhsT_scale=lhsT_scale,
-                                    rhs=v_words[a][:, cols].bitcast(FP8X4), rhs_scale=(v_plane, v_plane1)[a][:, cols],
-                                    start=(a == 0), stop=(a == 1))
+                                    rhs=v_words[a][:, cols].bitcast(FP8X4),
+                                    rhs_scale=(v_plane, v_plane1)[a][:, cols], start=(a == 0), stop=(a == 1))
 
-        for t in range(PACK):
-            old = placed([P, S], F32, "old%d" % t, 4096 if t == 1 else 0)
-            nc.vector.tensor_copy(old[:], page[t][:].indirect(idx2[:]))
+        def larger_reading(t):
             for hf in range(S // HALF):
+                u = 2 * t + hf
                 cols = slice(hf * HALF, (hf + 1) * HALF)
-                unit = "%d_%d" % (t, hf)
-                a_ps, b_ps, d_ps = (bank([P, HALF], "a" + unit, hf), bank([P, HALF], "b" + unit, 2 + hf),
-                                    bank([P, HALF], "d" + unit, 4 + hf))
+                a_ps, b_ps = bank([P, HALF], "a%d" % u, hf), bank([P, HALF], "b%d" % u, 2 + hf)
                 first_product(b_ps, "w2", t, cols)
                 first_product(a_ps, "w1", t, cols)
-                first_product(d_ps, "w3", t, cols)
-                b_sb = placed([P, HALF], F32, "b_sb%d_%d" % (t, hf), 1024 * 56 + 2048 * hf)
+                b_sb = placed([P, HALF], F32, "b_sb%d" % u, (224, 228, 232, 236, 80, 84, 88, 92)[u] * KB // 2)
                 nc.scalar.copy(b_sb[:], b_ps[:])
+                larger[t, hf] = placed([P, HALF], F32, "larger%d" % u, (192, 196, 200, 204, 128, 132, 136, 140)[u] * KB // 2)
+                nc.vector.tensor_tensor(larger[t, hf][:], a_ps[:], b_sb[:], ALU.max)
+
+        def fetch_old(t):
+            old[t] = placed([P, S], F32, "old%d" % t, (128, 136, 144, 152)[t] * KB // 2)
+            nc.vector.tensor_copy(old[t][:], page[t][:].indirect(idx2[:]))
+
+        nc.sync.dma_start(idx[:], offs)
+        nc.sync.dma_start(idx2[:], offs2)
+        load_tab_scales()
+        load_tab(0)
+        nc.sync.dma_start(out=w2_in[:].bitcast(I32), in_=w2_words.rearrange("a p c -> p a c").bitcast(I32))
+        load_w2_scales()
+        load_weight("w1", w1, 0, 16 * KB)
+        load_tab(1)
+        nc.vector.tensor_copy(v_plane[:], tab_plane[:].indirect(idx[:]))
+        gather_words(0)
+        deal_w2_words()
+        deal_w2_scales()
+        quantise_weight("w1", 0, [(nc.vector.tensor_copy, 104 * KB)])
+        gather_words(1)
+        load_weight("w1", w1, 1, 24 * KB)
+        load_page(0, 48 * KB)
+        move_scale_rows()
+        nc.sync.dma_start(out=gv_sb[:], in_=gv.rearrange("(p t) -> p t", t=PACK))
+        load_weight("w3", w3, 0, 32 * KB)
+        load_page(1, 56 * KB)
+        load_weight("w3", w3, 1, 40 * KB)
+        load_page(2, 0)
+        load_page(3, 16 * KB)
+        nc.sync.dma_start(idx3[:], offs3)
+        load_weight("w4", w4, 0, 8 * KB)
+        load_w5()
+        quantise_weight("w1", 1, [(nc.vector.tensor_copy, 108 * KB)])
+        fetch_old(0)
+        larger_reading(0)
+        larger_reading(1)
+        quantise_weight("w3", 0, [(nc.scalar.copy, 104 * KB)])
+        fetch_old(1)
+        quantise_weight("w3", 1, [(nc.scalar.copy, 108 * KB), (nc.scalar.copy, 110 * KB)])
+        fetch_old(2)
+        fetch_old(3)
+
+        for t in range(PACK):
+            h = kept([P, S], F32, "h")
+            for hf in range(S // HALF):
+                cols = slice(hf * HALF, (hf + 1) * HALF)
+                d_ps = bank([P, HALF], "d%d_%d" % (t, hf), 4 + hf)
+                first_product(d_ps, "w3", t, cols)
                 th = work.tile([P, HALF], F32, name="th")
                 nc.scalar.activation(th[:], d_ps[:], ACT.Tanh)
-                larger = placed([P, HALF], F32, "larger%d_%d" % (t, hf), 16384 + 2048 * hf)
-                nc.vector.tensor_tensor(larger[:], a_ps[:], b_sb[:], ALU.max)
                 bounded = work.tile([P, HALF], F32, name="bounded")
                 nc.scalar.activation(bounded[:], th[:], ACT.Copy, scale=gv_sb[:, t : t + 1])
-                h = work.tile([P, HALF], F32, name="h")
-                nc.gpsimd.tensor_tensor(h[:], larger[:], bounded[:], ALU.add)
-                new = placed([P, HALF], F32, "new%d_%d" % (t, hf), 20480 + 2048 * hf)
-                nc.vector.tensor_tensor(new[:], h[:], old[:, cols], ALU.max)
-                nc.vector.tensor_copy(page[t][:].indirect(idx2[:, hf * HALF // 16 : (hf + 1) * HALF // 16]), new[:])
+                nc.gpsimd.tensor_tensor(h[:, cols], larger[t, hf][:], bounded[:], ALU.add)
+            new = placed([P, S], F32, "new%d" % t, (80 + 4 * (t % 2)) * KB)
+            nc.vector.tensor_tensor(new[:], h[:], old[t][:], ALU.max)
+            if t + 2 < PACK:
+                larger_reading(t + 2)
+            nc.vector.tensor_copy(page[t][:].indirect(idx2[:]), new[:])
             if t == 1:
-                w5_plane_in = placed([P, N], U8, "w5_plane_in", 4096)
-                w5_in = placed([P, N], I32, "w5_in", 4608)
-                load_weight("w4", w4, 0, placed([P, PACK, N], F32, "raw_w4", 6656))
-                nc.sync.dma_start(out=w5_in[:], in_=w5_words[0].rearrange("p c i -> p (c i)").bitcast(I32))
-                nc.gpsimd.memset(w5_plane_in[:].bitcast(I32), 0)
-                for q in range(4):
-                    nc.sync.dma_start(out=w5_plane_in[32 * q : 32 * q + 4, :].bitcast(I32),
-                                      in_=w5_scales[0, 4 * q : 4 * q + 4, :].bitcast(I32))
-            if t == 2:
-                quantise_weight("w4", 0, [(nc.scalar.copy, 1024 * 24)])
+                quantise_weight("w4", 0, [(nc.scalar.copy, 104 * KB)])
                 w5_codes = kept([P, N], I32, "w5_codes")
                 nc.gpsimd.tensor_copy(w5_codes[:].rearrange("p (t m) -> p m t", t=PACK),
                                       w5_in[:].rearrange("p (m t) -> p m t", t=PACK))
@@ -193,16 +226,16 @@ def tile_list_sighting_credibility_page_kernel(
 
         def look_up(c):
             n, m0 = CHUNKS[c], starts[c]
-            picked = placed([P, PACK, n], BF16, "picked%d" % c, 69632 + 2048 if c == 3 else 20480 + 2048 * (c % 2))
+            picked = placed([P, PACK, n], BF16, "picked%d" % c, (80, 84, 80, 90)[c] * KB)
             for t in range(PACK):
                 nc.vector.tensor_copy(picked[:, t, :], page[t][:].indirect(idx3[:, m0 // 16 : (m0 + n) // 16]))
-            x_bf[c] = kept([P, PACK * n], BF16, "x_bf%d" % c)
+            x_bf[c] = placed([P, PACK * n], BF16, "x_bf%d" % c, (96, 98, 100, 102)[c] * KB)
             nc.scalar.copy(x_bf[c][:].rearrange("p (g i t) -> p g t i", i=4, t=PACK),
                            picked[:].rearrange("p t (g i) -> p g t i", i=4))
 
         def quantise_x(c):
             n = CHUNKS[c]
-            x_codes[c] = kept([P, n], U32, "x_codes%d" % c)
+            x_codes[c] = placed([P, n], U32, "x_codes%d" % c, (100, 102, 104, 105)[c] * KB)
             x_plane[c] = kept([P, n], U8, "x_plane%d" % c)
             nc.vector.quantize_mx(out=x_codes[c][:].bitcast(FP8X4), scales=x_plane[c][:], in_=x_bf[c][:])
 
@@ -218,7 +251,7 @@ def tile_list_sighting_credibility_page_kernel(
                         nc.tensor.matmul_mx(out=ps[:, i, :], lhsT=words[:, rows].bitcast(FP8X4),
                                             lhsT_scale=plane[:, rows], rhs=x_codes[c][:].bitcast(FP8X4),
                                             rhs_scale=x_plane[c][:], start=True, stop=True)
-                gate[c, t0] = placed([P, per_bank, n], F32, "gate%d_%d" % (c, t0), 69632 + 4096 * (c % 2) + 1024 * t0)
+                gate[c, t0] = placed([P, per_bank, n], F32, "gate%d_%d" % (c, t0), (88 + 4 * (c % 2) + t0) * KB)
                 nc.scalar.activation(gate[c, t0][:], f_ps[:], ACT.Sigmoid)
 
         def results(c):
@@ -243,5 +276,5 @@ def tile_list_sighting_credibility_page_kernel(
                 if 0 <= i - lag < len(CHUNKS):
                     step(i - lag)
         for q in range(4):
-            nc.sync.dma_start(out=out_2[0, 4 * q : 4 * q + 4, :].bitcast(I32),
-                              in_=y_plane[32 * q : 32 * q + 4, :].bitcast(I32))
+            (nc.sync, nc.scalar)[q % 2].dma_start(out=out_2[0, 4 * q : 4 * q + 4, :].bitcast(I32),
+                                                  in_=y_plane[32 * q : 32 * q + 4, :].bitcast(I32))

@@ -19,9 +19,28 @@ ACT = mybir.ActivationFunctionType
 P = 128
 PACK = 4
 PASS = P * PACK
-HALF = 512
+BANK = 512
+QUADS = 4
+CHUNK = 256
+CHUNKS = M // CHUNK
+RUN = 4
+SPARE_ROW = 16
+
 KB = 1024
-CHUNKS = [256, 256, 256, 256]
+TABLE_AT = (0, 8)
+RAW_AT = {("w1", 0): 16, ("w1", 1): 24, ("w3", 0): 32, ("w3", 1): 40, ("w4", 0): 8}
+PAGE_AT = (48, 56, 0, 16)
+OLD_AT = (64, 68, 72, 76)
+NEW_AT = (80, 84)
+LARGER_AT = (96, 98, 100, 102, 64, 66, 68, 70)
+B_AT = (112, 114, 116, 118, 40, 42, 44, 46)
+DEALT_AT = (104, 108)
+PICKED_AT = (80, 84, 80, 90)
+GATE_AT = (88, 92)
+X_BF_AT = (96, 98, 100, 102)
+X_CODES_AT = (100, 102, 104, 105)
+A_BANK, B_BANK, D_BANK = 0, 2, 4
+E_BANK, F_BANK = (0, 6), (2, 4)
 
 
 def tile_list_sighting_credibility_page_kernel(
@@ -33,17 +52,23 @@ def tile_list_sighting_credibility_page_kernel(
         lists = ctx.enter_context(tc.tile_pool(name="lists", bufs=1))
         keep = ctx.enter_context(tc.tile_pool(name="keep", bufs=1))
         work = ctx.enter_context(tc.tile_pool(name="work", bufs=2))
-        reuse = ctx.enter_context(tc.tile_pool(name="reuse", bufs=1))
+        shared = ctx.enter_context(tc.tile_pool(name="shared", bufs=1))
         psum = ctx.enter_context(tc.psum_pool(name="psum", bufs=1))
 
         def kept(shape, dtype, name):
             return keep.tile(shape, dtype, name=name, align_bytes=64)
 
-        def placed(shape, dtype, name, offset):
-            return reuse.tile(shape, dtype, name=name, align_bytes=64, offset=offset)
+        def placed(shape, dtype, name, kib):
+            return shared.tile(shape, dtype, name=name, align_bytes=64, offset=kib * KB)
 
         def bank(shape, name, number):
-            return psum.tile(shape, F32, name=name, offset=2048 * number)
+            return psum.tile(shape, F32, name=name, offset=number * BANK * 4)
+
+        def plane_rows(q):
+            return slice(32 * q, 32 * q + 4)
+
+        def scale_rows(q):
+            return slice(4 * q, 4 * q + 4)
 
         idx = lists.tile([P, S // 16], U16, name="idx")
         idx2 = lists.tile([P, S // 16], U16, name="idx2")
@@ -53,14 +78,11 @@ def tile_list_sighting_credibility_page_kernel(
         v_plane1 = kept([P, S], U8, "v_plane1")
         w2_plane_in = kept([P, 2, H], U8, "w2_plane_in")
         w5_plane_in = kept([P, N], U8, "w5_plane_in")
-        nc.gpsimd.memset(tab_plane[:, : T // 2].bitcast(I32), 0)
-        nc.vector.memset(tab_plane[:, T // 2 :].bitcast(I32), 0)
+        nc.vector.memset(tab_plane[:].bitcast(I32), 0)
         nc.gpsimd.memset(w2_plane_in[:].bitcast(I32), 0)
         nc.gpsimd.memset(v_plane1[:].bitcast(I32), 0)
         nc.gpsimd.memset(w5_plane_in[:].bitcast(I32), 0)
 
-        tab, raw, page, codes, planes, larger, old = {}, {}, {}, {}, {}, {}, {}
-        page_rows = page0.rearrange("(p t) c -> p t c", t=PACK)
         w2_in = kept([P, 2, 2 * H], U8, "w2_in")
         w5_in = kept([P, N], I32, "w5_in")
         gv_sb = kept([P, PACK], F32, "gv_sb")
@@ -68,64 +90,37 @@ def tile_list_sighting_credibility_page_kernel(
         v_plane = kept([P, S], U8, "v_plane")
         w2_codes = kept([P, 2, 2 * H], U8, "w2_codes")
         w2_plane = kept([P, 2, H], U8, "w2_plane")
+        tab, raw, page, codes, planes, larger, old = {}, {}, {}, {}, {}, {}, {}
+        page_rows = page0.rearrange("(p t) c -> p t c", t=PACK)
 
-        def load_tab(a):
-            tab[a] = placed([P, T], I32, "tab%d" % a, 8 * a * KB)
+        def load_table(a):
+            tab[a] = placed([P, T], I32, "tab%d" % a, TABLE_AT[a])
             nc.sync.dma_start(out=tab[a][:], in_=tab_words[a].rearrange("p t i -> p (t i)").bitcast(I32))
 
-        def load_tab_scales():
-            for q in range(4):
-                nc.sync.dma_start(out=tab_plane[32 * q : 32 * q + 4, :].bitcast(I32),
-                                  in_=tab_scales[0, 4 * q : 4 * q + 4, :].bitcast(I32))
-            nc.sync.dma_start(out=tab_plane[16:32, :].bitcast(I32), in_=tab_scales[1].bitcast(I32))
-
-        def load_w2_scales():
-            for q in range(4):
-                nc.sync.dma_start(out=w2_plane_in[32 * q : 32 * q + 4, :, :].bitcast(I32),
-                                  in_=w2_scales[:, 4 * q : 4 * q + 4, :].rearrange("a r c -> r a c").bitcast(I32))
-
-        def load_w5():
-            nc.sync.dma_start(out=w5_in[:], in_=w5_words[0].rearrange("p c i -> p (c i)").bitcast(I32))
-            for q in range(4):
-                nc.sync.dma_start(out=w5_plane_in[32 * q : 32 * q + 4, :].bitcast(I32),
-                                  in_=w5_scales[0, 4 * q : 4 * q + 4, :].bitcast(I32))
-
-        def load_weight(name, w, a, offset):
-            raw[name, a] = placed([P, PACK, H], F32, "raw_%s_%d" % (name, a), offset)
+        def load_weight(name, w, a):
+            raw[name, a] = placed([P, PACK, H], F32, "raw_%s_%d" % (name, a), RAW_AT[name, a])
             nc.sync.dma_start(out=raw[name, a][:],
                               in_=w[a * PASS : (a + 1) * PASS, :].rearrange("(p j) c -> p j c", j=PACK))
 
-        def load_page(t, offset):
-            page[t] = placed([P, T2], F32, "page%d" % t, offset)
+        def load_page(t):
+            page[t] = placed([P, T2], F32, "page%d" % t, PAGE_AT[t])
             nc.sync.dma_start(out=page[t][:], in_=page_rows[:, t, :])
 
         def gather_words(a):
             nc.vector.tensor_copy(v_words[a][:], tab[a][:].bitcast(U32).indirect(idx[:]))
 
-        def move_scale_rows():
-            for q in range(4):
-                nc.sync.dma_start(out=v_plane1[32 * q : 32 * q + 4, :].bitcast(I32),
-                                  in_=v_plane[16 + 4 * q : 20 + 4 * q, :].bitcast(I32))
-
-        def quantise_weight(name, a, parts):
+        def quantise_weight(name, a, kib, parts=1):
             codes[name, a] = kept([P, H], U32, "codes_%s_%d" % (name, a))
             planes[name, a] = kept([P, H], U8, "plane_%s_%d" % (name, a))
-            slices = PACK // len(parts)
-            for i, (copy, offset) in enumerate(parts):
-                dealt = placed([P, slices * PASS], BF16, "dealt_%s_%d_%d" % (name, a, i), offset)
-                copy(dealt[:].rearrange("p (t m j) -> p m j t", t=slices, j=PACK),
-                     raw[name, a][:].rearrange("p j (m t) -> p m j t", t=PACK)[:, :, :, i * slices : (i + 1) * slices])
+            slices = PACK // parts
+            for i in range(parts):
+                dealt = placed([P, slices * PASS], BF16, "dealt_%s_%d_%d" % (name, a, i), kib + i * slices)
+                nc.scalar.copy(
+                    dealt[:].rearrange("p (t m j) -> p m j t", t=slices, j=PACK),
+                    raw[name, a][:].rearrange("p j (m t) -> p m j t", t=PACK)[:, :, :, i * slices : (i + 1) * slices])
                 cols = slice(i * slices * P, (i + 1) * slices * P)
                 nc.vector.quantize_mx(out=codes[name, a][:, cols].bitcast(FP8X4), scales=planes[name, a][:, cols],
                                       in_=dealt[:])
-
-        def deal_w2_words():
-            nc.vector.tensor_copy(w2_codes[:].bitcast(U16).rearrange("p a (t m) -> p a t m", t=PACK),
-                                  w2_in[:].bitcast(U16).rearrange("p a (m t) -> p a t m", t=PACK))
-
-        def deal_w2_scales():
-            nc.vector.tensor_copy(w2_plane[:].rearrange("p a (t m) -> p a t m", t=PACK),
-                                  w2_plane_in[:].rearrange("p a (m t) -> p a t m", t=PACK))
 
         def first_product(out, name, t, cols):
             rows = slice(t * P, (t + 1) * P)
@@ -141,75 +136,89 @@ def tile_list_sighting_credibility_page_kernel(
                                     rhs_scale=(v_plane, v_plane1)[a][:, cols], start=(a == 0), stop=(a == 1))
 
         def larger_reading(t):
-            for hf in range(S // HALF):
-                u = 2 * t + hf
-                cols = slice(hf * HALF, (hf + 1) * HALF)
-                a_ps, b_ps = bank([P, HALF], "a%d" % u, hf), bank([P, HALF], "b%d" % u, 2 + hf)
+            for half in range(S // BANK):
+                u = 2 * t + half
+                cols = slice(half * BANK, (half + 1) * BANK)
+                a_ps, b_ps = bank([P, BANK], "a%d" % u, A_BANK + half), bank([P, BANK], "b%d" % u, B_BANK + half)
                 first_product(b_ps, "w2", t, cols)
                 first_product(a_ps, "w1", t, cols)
-                b_sb = placed([P, HALF], F32, "b_sb%d" % u, (224, 228, 232, 236, 80, 84, 88, 92)[u] * KB // 2)
+                b_sb = placed([P, BANK], F32, "b_sb%d" % u, B_AT[u])
                 nc.scalar.copy(b_sb[:], b_ps[:])
-                larger[t, hf] = placed([P, HALF], F32, "larger%d" % u, (192, 196, 200, 204, 128, 132, 136, 140)[u] * KB // 2)
-                nc.vector.tensor_tensor(larger[t, hf][:], a_ps[:], b_sb[:], ALU.max)
+                larger[t, half] = placed([P, BANK], F32, "larger%d" % u, LARGER_AT[u])
+                nc.vector.tensor_tensor(larger[t, half][:], a_ps[:], b_sb[:], ALU.max)
 
         def fetch_old(t):
-            old[t] = placed([P, S], F32, "old%d" % t, (128, 136, 144, 152)[t] * KB // 2)
+            old[t] = placed([P, S], F32, "old%d" % t, OLD_AT[t])
             nc.vector.tensor_copy(old[t][:], page[t][:].indirect(idx2[:]))
 
         nc.sync.dma_start(idx[:], offs)
-        nc.sync.dma_start(idx2[:], offs2)
-        load_tab_scales()
-        load_tab(0)
+        load_table(0)
         nc.sync.dma_start(out=w2_in[:].bitcast(I32), in_=w2_words.rearrange("a p c -> p a c").bitcast(I32))
-        load_w2_scales()
-        load_weight("w1", w1, 0, 16 * KB)
-        load_tab(1)
-        nc.vector.tensor_copy(v_plane[:], tab_plane[:].indirect(idx[:]))
+        for q in range(QUADS):
+            nc.sync.dma_start(out=tab_plane[plane_rows(q), :].bitcast(I32),
+                              in_=tab_scales[0, scale_rows(q), :].bitcast(I32))
+        nc.sync.dma_start(out=tab_plane[SPARE_ROW : SPARE_ROW + 16, :].bitcast(I32), in_=tab_scales[1].bitcast(I32))
+        load_weight("w1", w1, 0)
+        load_table(1)
+        nc.sync.dma_start(idx2[:], offs2)
+        for q in range(QUADS):
+            nc.sync.dma_start(out=w2_plane_in[plane_rows(q), :, :].bitcast(I32),
+                              in_=w2_scales[:, scale_rows(q), :].rearrange("a r c -> r a c").bitcast(I32))
+
         gather_words(0)
-        deal_w2_words()
-        deal_w2_scales()
-        quantise_weight("w1", 0, [(nc.vector.tensor_copy, 104 * KB)])
+        nc.vector.tensor_copy(w2_codes[:].bitcast(U16).rearrange("p a (t m) -> p a t m", t=PACK),
+                              w2_in[:].bitcast(U16).rearrange("p a (m t) -> p a t m", t=PACK))
+        nc.vector.tensor_copy(v_plane[:], tab_plane[:].indirect(idx[:]))
+        quantise_weight("w1", 0, DEALT_AT[0])
+        nc.vector.tensor_copy(w2_plane[:].rearrange("p a (t m) -> p a t m", t=PACK),
+                              w2_plane_in[:].rearrange("p a (m t) -> p a t m", t=PACK))
         gather_words(1)
-        load_weight("w1", w1, 1, 24 * KB)
-        load_page(0, 48 * KB)
-        move_scale_rows()
+
+        load_weight("w1", w1, 1)
+        load_page(0)
+        for q in range(QUADS):
+            nc.sync.dma_start(out=v_plane1[plane_rows(q), :].bitcast(I32),
+                              in_=v_plane[SPARE_ROW + 4 * q : SPARE_ROW + 4 * q + 4, :].bitcast(I32))
         nc.sync.dma_start(out=gv_sb[:], in_=gv.rearrange("(p t) -> p t", t=PACK))
-        load_weight("w3", w3, 0, 32 * KB)
-        load_page(1, 56 * KB)
-        load_weight("w3", w3, 1, 40 * KB)
-        load_page(2, 0)
-        load_page(3, 16 * KB)
+        load_page(1)
+        load_weight("w3", w3, 0)
+        load_weight("w3", w3, 1)
+        load_page(2)
+        load_page(3)
         nc.sync.dma_start(idx3[:], offs3)
-        load_weight("w4", w4, 0, 8 * KB)
-        load_w5()
-        quantise_weight("w1", 1, [(nc.vector.tensor_copy, 108 * KB)])
-        fetch_old(0)
-        larger_reading(0)
-        larger_reading(1)
-        quantise_weight("w3", 0, [(nc.scalar.copy, 104 * KB)])
-        fetch_old(1)
-        quantise_weight("w3", 1, [(nc.scalar.copy, 108 * KB), (nc.scalar.copy, 110 * KB)])
-        fetch_old(2)
-        fetch_old(3)
+        load_weight("w4", w4, 0)
+        nc.sync.dma_start(out=w5_in[:], in_=w5_words[0].rearrange("p c i -> p (c i)").bitcast(I32))
+        for q in range(QUADS):
+            nc.sync.dma_start(out=w5_plane_in[plane_rows(q), :].bitcast(I32),
+                              in_=w5_scales[0, scale_rows(q), :].bitcast(I32))
+
+        quantise_weight("w1", 1, DEALT_AT[1])
+        for t in range(2):
+            fetch_old(t)
+            larger_reading(t)
+        quantise_weight("w3", 0, DEALT_AT[0])
+        quantise_weight("w3", 1, DEALT_AT[1], parts=2)
+        for t in range(2, PACK):
+            fetch_old(t)
 
         for t in range(PACK):
             h = kept([P, S], F32, "h")
-            for hf in range(S // HALF):
-                cols = slice(hf * HALF, (hf + 1) * HALF)
-                d_ps = bank([P, HALF], "d%d_%d" % (t, hf), 4 + hf)
+            for half in range(S // BANK):
+                cols = slice(half * BANK, (half + 1) * BANK)
+                d_ps = bank([P, BANK], "d%d_%d" % (t, half), D_BANK + half)
                 first_product(d_ps, "w3", t, cols)
-                th = work.tile([P, HALF], F32, name="th")
+                th = work.tile([P, BANK], F32, name="th")
                 nc.scalar.activation(th[:], d_ps[:], ACT.Tanh)
-                bounded = work.tile([P, HALF], F32, name="bounded")
+                bounded = work.tile([P, BANK], F32, name="bounded")
                 nc.scalar.activation(bounded[:], th[:], ACT.Copy, scale=gv_sb[:, t : t + 1])
-                nc.gpsimd.tensor_tensor(h[:, cols], larger[t, hf][:], bounded[:], ALU.add)
-            new = placed([P, S], F32, "new%d" % t, (80 + 4 * (t % 2)) * KB)
+                nc.gpsimd.tensor_tensor(h[:, cols], larger[t, half][:], bounded[:], ALU.add)
+            new = placed([P, S], F32, "new%d" % t, NEW_AT[t % 2])
             nc.vector.tensor_tensor(new[:], h[:], old[t][:], ALU.max)
             if t + 2 < PACK:
                 larger_reading(t + 2)
             nc.vector.tensor_copy(page[t][:].indirect(idx2[:]), new[:])
             if t == 1:
-                quantise_weight("w4", 0, [(nc.scalar.copy, 104 * KB)])
+                quantise_weight("w4", 0, DEALT_AT[0])
                 w5_codes = kept([P, N], I32, "w5_codes")
                 nc.gpsimd.tensor_copy(w5_codes[:].rearrange("p (t m) -> p m t", t=PACK),
                                       w5_in[:].rearrange("p (m t) -> p m t", t=PACK))
@@ -221,60 +230,58 @@ def tile_list_sighting_credibility_page_kernel(
         y_plane = kept([P, M], U8, "y_plane")
         out_rows = out_0.rearrange("(p t) m -> p t m", t=PACK)
         out_words = out_1[0].rearrange("p m i -> p (m i)").bitcast(I32)
-        starts = [sum(CHUNKS[:c]) for c in range(len(CHUNKS))]
+        per_bank = BANK // CHUNK
         x_bf, x_codes, x_plane, e_ps, gate, y_bf = {}, {}, {}, {}, {}, {}
 
+        def interleave(copy, dst, src):
+            copy(dst[:].rearrange("p (g i t) -> p g t i", i=RUN, t=PACK),
+                 src[:].rearrange("p t (g i) -> p g t i", i=RUN))
+
         def look_up(c):
-            n, m0 = CHUNKS[c], starts[c]
-            picked = placed([P, PACK, n], BF16, "picked%d" % c, (80, 84, 80, 90)[c] * KB)
+            picked = placed([P, PACK, CHUNK], BF16, "picked%d" % c, PICKED_AT[c])
+            entries = idx3[:, c * CHUNK // 16 : (c + 1) * CHUNK // 16]
             for t in range(PACK):
-                nc.vector.tensor_copy(picked[:, t, :], page[t][:].indirect(idx3[:, m0 // 16 : (m0 + n) // 16]))
-            x_bf[c] = placed([P, PACK * n], BF16, "x_bf%d" % c, (96, 98, 100, 102)[c] * KB)
-            nc.scalar.copy(x_bf[c][:].rearrange("p (g i t) -> p g t i", i=4, t=PACK),
-                           picked[:].rearrange("p t (g i) -> p g t i", i=4))
+                nc.vector.tensor_copy(picked[:, t, :], page[t][:].indirect(entries))
+            x_bf[c] = placed([P, PACK * CHUNK], BF16, "x_bf%d" % c, X_BF_AT[c])
+            interleave(nc.scalar.copy, x_bf[c], picked)
 
         def quantise_x(c):
-            n = CHUNKS[c]
-            x_codes[c] = placed([P, n], U32, "x_codes%d" % c, (100, 102, 104, 105)[c] * KB)
-            x_plane[c] = kept([P, n], U8, "x_plane%d" % c)
+            x_codes[c] = placed([P, CHUNK], U32, "x_codes%d" % c, X_CODES_AT[c])
+            x_plane[c] = kept([P, CHUNK], U8, "x_plane%d" % c)
             nc.vector.quantize_mx(out=x_codes[c][:].bitcast(FP8X4), scales=x_plane[c][:], in_=x_bf[c][:])
 
         def products(c):
-            n = CHUNKS[c]
-            per_bank = HALF // n
-            for t0 in range(0, PACK, per_bank):
-                f_ps = bank([P, per_bank, n], "f%d_%d" % (c, t0), 2 + 2 * (c % 2) + t0 // per_bank)
-                e_ps[c, t0] = bank([P, per_bank, n], "e%d_%d" % (c, t0), 6 * (c % 2) + t0 // per_bank)
-                for ps, words, plane in ((f_ps, w5_codes, w5_plane), (e_ps[c, t0], codes["w4", 0], planes["w4", 0])):
+            for b in range(PACK // per_bank):
+                f_ps = bank([P, per_bank, CHUNK], "f%d_%d" % (c, b), F_BANK[c % 2] + b)
+                e_ps[c, b] = bank([P, per_bank, CHUNK], "e%d_%d" % (c, b), E_BANK[c % 2] + b)
+                for ps, words, plane in ((f_ps, w5_codes, w5_plane), (e_ps[c, b], codes["w4", 0], planes["w4", 0])):
                     for i in range(per_bank):
-                        rows = slice((t0 + i) * P, (t0 + i + 1) * P)
+                        rows = slice((b * per_bank + i) * P, (b * per_bank + i + 1) * P)
                         nc.tensor.matmul_mx(out=ps[:, i, :], lhsT=words[:, rows].bitcast(FP8X4),
                                             lhsT_scale=plane[:, rows], rhs=x_codes[c][:].bitcast(FP8X4),
                                             rhs_scale=x_plane[c][:], start=True, stop=True)
-                gate[c, t0] = placed([P, per_bank, n], F32, "gate%d_%d" % (c, t0), (88 + 4 * (c % 2) + t0) * KB)
-                nc.scalar.activation(gate[c, t0][:], f_ps[:], ACT.Sigmoid)
+                gate[c, b] = placed([P, per_bank, CHUNK], F32, "gate%d_%d" % (c, b), GATE_AT[c % 2] + 2 * b)
+                nc.scalar.activation(gate[c, b][:], f_ps[:], ACT.Sigmoid)
 
         def results(c):
-            n, m0 = CHUNKS[c], starts[c]
-            per_bank = HALF // n
-            y = kept([P, PACK, n], F32, "y%d" % c)
-            for t0 in range(0, PACK, per_bank):
-                nc.vector.tensor_tensor(y[:, t0 : t0 + per_bank, :], e_ps[c, t0][:], gate[c, t0][:], ALU.add)
-            nc.sync.dma_start(out=out_rows[:, :, m0 : m0 + n], in_=y[:])
-            y_bf[c] = kept([P, PACK * n], BF16, "y_bf%d" % c)
-            copy = nc.vector.tensor_copy if c == len(CHUNKS) - 1 else nc.scalar.copy
-            copy(y_bf[c][:].rearrange("p (g i t) -> p g t i", i=4, t=PACK),
-                 y[:].rearrange("p t (g i) -> p g t i", i=4))
+            y = kept([P, PACK, CHUNK], F32, "y%d" % c)
+            for b in range(PACK // per_bank):
+                nc.vector.tensor_tensor(y[:, b * per_bank : (b + 1) * per_bank, :], e_ps[c, b][:], gate[c, b][:],
+                                        ALU.add)
+            nc.sync.dma_start(out=out_rows[:, :, c * CHUNK : (c + 1) * CHUNK], in_=y[:])
+            y_bf[c] = kept([P, PACK * CHUNK], BF16, "y_bf%d" % c)
+            interleave(nc.vector.tensor_copy if c == CHUNKS - 1 else nc.scalar.copy, y_bf[c], y)
 
         def quantise_y(c):
-            cols = slice(starts[c], starts[c] + CHUNKS[c])
+            cols = slice(c * CHUNK, (c + 1) * CHUNK)
             nc.vector.quantize_mx(out=y_codes[:, cols].bitcast(FP8X4), scales=y_plane[:, cols], in_=y_bf[c][:])
             nc.sync.dma_start(out=out_words[:, cols], in_=y_codes[:, cols])
 
-        for i in range(len(CHUNKS) + 4):
-            for step, lag in ((results, 3), (look_up, 0), (quantise_x, 1), (products, 1), (quantise_y, 4)):
-                if 0 <= i - lag < len(CHUNKS):
+        pipeline = ((results, 3), (look_up, 0), (quantise_x, 1), (products, 1), (quantise_y, 4))
+        for i in range(CHUNKS + 4):
+            for step, lag in pipeline:
+                if 0 <= i - lag < CHUNKS:
                     step(i - lag)
-        for q in range(4):
-            (nc.sync, nc.scalar)[q % 2].dma_start(out=out_2[0, 4 * q : 4 * q + 4, :].bitcast(I32),
-                                                  in_=y_plane[32 * q : 32 * q + 4, :].bitcast(I32))
+        for q in range(QUADS):
+            (nc.sync, nc.scalar)[q % 2].dma_start(out=out_2[0, scale_rows(q), :].bitcast(I32),
+                                                  in_=y_plane[plane_rows(q), :].bitcast(I32))

@@ -33,13 +33,13 @@ PAGE_AT = (48, 56, 0, 16)
 OLD_AT = (64, 68, 72, 76)
 NEW_AT = (80, 84)
 LARGER_AT = (96, 98, 100, 102, 64, 66, 68, 70)
-B_AT = (112, 114, 116, 118, 40, 42, 44, 46)
+B_AT = (112, 114, 116, 118, 96, 98, 100, 102)
 DEALT_AT = (104, 108)
 PICKED_AT = (80, 84, 80, 90)
 GATE_AT = (88, 92)
 X_BF_AT = (96, 98, 100, 102)
 X_CODES_AT = (100, 102, 104, 105)
-A_BANK, B_BANK, D_BANK = 0, 2, 4
+A_BANKS, B_BANK, D_BANK = (0, 1, 6, 7), 2, 4
 E_BANK, F_BANK = (0, 6), (2, 4)
 
 
@@ -73,6 +73,11 @@ def tile_list_sighting_credibility_page_kernel(
         idx = lists.tile([P, S // 16], U16, name="idx")
         idx2 = lists.tile([P, S // 16], U16, name="idx2")
         idx3 = lists.tile([P, M // 16], U16, name="idx3")
+
+        warm_in = kept([P, 1], F32, "warm_in")
+        warm_out = kept([P, 1], F32, "warm_out")
+        nc.gpsimd.memset(warm_in[:], 0.0)
+        nc.scalar.activation(warm_out[:], warm_in[:], ACT.Sigmoid)
 
         tab_plane = kept([P, T], U8, "tab_plane")
         v_plane1 = kept([P, S], U8, "v_plane1")
@@ -139,7 +144,7 @@ def tile_list_sighting_credibility_page_kernel(
             for half in range(S // BANK):
                 u = 2 * t + half
                 cols = slice(half * BANK, (half + 1) * BANK)
-                a_ps, b_ps = bank([P, BANK], "a%d" % u, A_BANK + half), bank([P, BANK], "b%d" % u, B_BANK + half)
+                a_ps, b_ps = bank([P, BANK], "a%d" % u, A_BANKS[u % 4]), bank([P, BANK], "b%d" % u, B_BANK + half)
                 first_product(b_ps, "w2", t, cols)
                 first_product(a_ps, "w1", t, cols)
                 b_sb = placed([P, BANK], F32, "b_sb%d" % u, B_AT[u])

from contextlib import ExitStack

import concourse.mybir as mybir

K, H, N, T, S, T2, M = 1024, 512, 512, 2048, 1024, 2048, 1024
FLOPS = 2 * (3 * K * H * S + 2 * H * N * M)

F32 = mybir.dt.float32
BF16 = mybir.dt.bfloat16
I32 = mybir.dt.int32
U32 = mybir.dt.uint32
U16 = mybir.dt.uint16
U8 = mybir.dt.uint8
FP8X4 = mybir.dt.float8_e4m3fn_x4
FP4X4 = mybir.dt.float4_e2m1fn_x4
ALU = mybir.AluOpType
ACT = mybir.ActivationFunctionType

P = 128
PACK = 4
PASS = P * PACK
BANK = 512
QUADS = 4
CHUNK = 256
CHUNKS = M // CHUNK
RUN = 4
SPARE_ROW = 16

KB = 1024
TABLE_AT = (0, 8)
RAW_AT = {("w1", 0): 16, ("w1", 1): 24, ("w3", 0): 32, ("w3", 1): 40, ("w4", 0): 8}
PAGE_AT = (48, 56, 0, 16)
OLD_AT = (64, 68, 72, 76)
NEW_AT = (80, 84)
LARGER_AT = (96, 98, 100, 102, 64, 66, 68, 70)
B_AT = (112, 114, 116, 118, 96, 98, 100, 102)
DEALT_AT = (104, 108)
PICKED_AT = (80, 84, 80, 90)
GATE_AT = (88, 92)
X_BF_AT = (96, 98, 100, 102)
X_CODES_AT = (100, 102, 104, 105)
A_BANKS, B_BANK, D_BANK = (0, 1, 6, 7), 2, 4
E_BANK, F_BANK = (0, 6), (2, 4)


def tile_list_sighting_credibility_page_kernel(
    tc, tab_words, tab_scales, offs, offs2, offs3, w1, w2_words, w2_scales, w3, gv, page0, w4,
    w5_words, w5_scales, out_0, out_1, out_2,
):
    nc = tc.nc
    with ExitStack() as ctx:
        lists = ctx.enter_context(tc.tile_pool(name="lists", bufs=1))
        keep = ctx.enter_context(tc.tile_pool(name="keep", bufs=1))
        work = ctx.enter_context(tc.tile_pool(name="work", bufs=2))
        shared = ctx.enter_context(tc.tile_pool(name="shared", bufs=1))
        psum = ctx.enter_context(tc.psum_pool(name="psum", bufs=1))

        def kept(shape, dtype, name):
            return keep.tile(shape, dtype, name=name, align_bytes=64)

        def placed(shape, dtype, name, kib):
            return shared.tile(shape, dtype, name=name, align_bytes=64, offset=kib * KB)

        def bank(shape, name, number):
            return psum.tile(shape, F32, name=name, offset=number * BANK * 4)

        def plane_rows(q):
            return slice(32 * q, 32 * q + 4)

        def scale_rows(q):
            return slice(4 * q, 4 * q + 4)

        idx = lists.tile([P, S // 16], U16, name="idx")
        idx2 = lists.tile([P, S // 16], U16, name="idx2")
        idx3 = lists.tile([P, M // 16], U16, name="idx3")

        warm_in = kept([P, 1], F32, "warm_in")
        warm_out = kept([P, 1], F32, "warm_out")
        nc.gpsimd.memset(warm_in[:], 0.0)
        nc.scalar.activation(warm_out[:], warm_in[:], ACT.Sigmoid)

        tab_plane = kept([P, T], U8, "tab_plane")
        v_plane1 = kept([P, S], U8, "v_plane1")
        w2_plane_in = kept([P, 2, H], U8, "w2_plane_in")
        w5_plane_in = kept([P, N], U8, "w5_plane_in")
        nc.vector.memset(tab_plane[:].bitcast(I32), 0)
        nc.gpsimd.memset(w2_plane_in[:].bitcast(I32), 0)
        nc.gpsimd.memset(v_plane1[:].bitcast(I32), 0)
        nc.gpsimd.memset(w5_plane_in[:].bitcast(I32), 0)

        w2_in = kept([P, 2, 2 * H], U8, "w2_in")
        w5_in = kept([P, N], I32, "w5_in")
        gv_sb = kept([P, PACK], F32, "gv_sb")
        v_words = [kept([P, S], U32, "v_words%d" % a) for a in range(2)]
        v_plane = kept([P, S], U8, "v_plane")
        w2_codes = kept([P, 2, 2 * H], U8, "w2_codes")
        w2_plane = kept([P, 2, H], U8, "w2_plane")
        tab, raw, page, codes, planes, larger, old = {}, {}, {}, {}, {}, {}, {}
        page_rows = page0.rearrange("(p t) c -> p t c", t=PACK)

        def load_table(a):
            tab[a] = placed([P, T], I32, "tab%d" % a, TABLE_AT[a])
            nc.sync.dma_start(out=tab[a][:], in_=tab_words[a].rearrange("p t i -> p (t i)").bitcast(I32))

        def load_weight(name, w, a):
            raw[name, a] = placed([P, PACK, H], F32, "raw_%s_%d" % (name, a), RAW_AT[name, a])
            nc.sync.dma_start(out=raw[name, a][:],
                              in_=w[a * PASS : (a + 1) * PASS, :].rearrange("(p j) c -> p j c", j=PACK))

        def load_page(t):
            page[t] = placed([P, T2], F32, "page%d" % t, PAGE_AT[t])
            nc.sync.dma_start(out=page[t][:], in_=page_rows[:, t, :])

        def gather_words(a):
            nc.vector.tensor_copy(v_words[a][:], tab[a][:].bitcast(U32).indirect(idx[:]))

        def quantise_weight(name, a, kib, parts=1):
            codes[name, a] = kept([P, H], U32, "codes_%s_%d" % (name, a))
            planes[name, a] = kept([P, H], U8, "plane_%s_%d" % (name, a))
            slices = PACK // parts
            for i in range(parts):
                dealt = placed([P, slices * PASS], BF16, "dealt_%s_%d_%d" % (name, a, i), kib + i * slices)
                nc.scalar.copy(
                    dealt[:].rearrange("p (t m j) -> p m j t", t=slices, j=PACK),
                    raw[name, a][:].rearrange("p j (m t) -> p m j t", t=PACK)[:, :, :, i * slices : (i + 1) * slices])
                cols = slice(i * slices * P, (i + 1) * slices * P)
                nc.vector.quantize_mx(out=codes[name, a][:, cols].bitcast(FP8X4), scales=planes[name, a][:, cols],
                                      in_=dealt[:])

        def first_product(out, name, t, cols):
            rows = slice(t * P, (t + 1) * P)
            for a in range(2):
                if name == "w2":
                    lhsT = w2_codes[:, a, 2 * t * P : 2 * (t + 1) * P].bitcast(FP4X4)
                    lhsT_scale = w2_plane[:, a, rows]
                else:
                    lhsT = codes[name, a][:, rows].bitcast(FP8X4)
                    lhsT_scale = planes[name, a][:, rows]
                nc.tensor.matmul_mx(out=out[:], lhsT=lhsT, lhsT_scale=lhsT_scale,
                                    rhs=v_words[a][:, cols].bitcast(FP8X4),
                                    rhs_scale=(v_plane, v_plane1)[a][:, cols], start=(a == 0), stop=(a == 1))

        def larger_reading(t):
            for half in range(S // BANK):
                u = 2 * t + half
                cols = slice(half * BANK, (half + 1) * BANK)
                a_ps, b_ps = bank([P, BANK], "a%d" % u, A_BANKS[u % 4]), bank([P, BANK], "b%d" % u, B_BANK + half)
                first_product(b_ps, "w2", t, cols)
                first_product(a_ps, "w1", t, cols)
                b_sb = placed([P, BANK], F32, "b_sb%d" % u, B_AT[u])
                nc.scalar.copy(b_sb[:], b_ps[:])
                larger[t, half] = placed([P, BANK], F32, "larger%d" % u, LARGER_AT[u])
                nc.vector.tensor_tensor(larger[t, half][:], a_ps[:], b_sb[:], ALU.max)

        def fetch_old(t):
            old[t] = placed([P, S], F32, "old%d" % t, OLD_AT[t])
            nc.vector.tensor_copy(old[t][:], page[t][:].indirect(idx2[:]))

        nc.sync.dma_start(idx[:], offs)
        load_table(0)
        nc.sync.dma_start(out=w2_in[:].bitcast(I32), in_=w2_words.rearrange("a p c -> p a c").bitcast(I32))
        for q in range(QUADS):
            nc.sync.dma_start(out=tab_plane[plane_rows(q), :].bitcast(I32),
                              in_=tab_scales[0, scale_rows(q), :].bitcast(I32))
        nc.sync.dma_start(out=tab_plane[SPARE_ROW : SPARE_ROW + 16, :].bitcast(I32), in_=tab_scales[1].bitcast(I32))
        load_weight("w1", w1, 0)
        load_table(1)
        nc.sync.dma_start(idx2[:], offs2)
        for q in range(QUADS):
            nc.sync.dma_start(out=w2_plane_in[plane_rows(q), :, :].bitcast(I32),
                              in_=w2_scales[:, scale_rows(q), :].rearrange("a r c -> r a c").bitcast(I32))

        gather_words(0)
        nc.vector.tensor_copy(w2_codes[:].bitcast(U16).rearrange("p a (t m) -> p a t m", t=PACK),
                              w2_in[:].bitcast(U16).rearrange("p a (m t) -> p a t m", t=PACK))
        nc.vector.tensor_copy(v_plane[:], tab_plane[:].indirect(idx[:]))
        quantise_weight("w1", 0, DEALT_AT[0])
        nc.vector.tensor_copy(w2_plane[:].rearrange("p a (t m) -> p a t m", t=PACK),
                              w2_plane_in[:].rearrange("p a (m t) -> p a t m", t=PACK))
        gather_words(1)

        load_weight("w1", w1, 1)
        load_page(0)
        for q in range(QUADS):
            nc.sync.dma_start(out=v_plane1[plane_rows(q), :].bitcast(I32),
                              in_=v_plane[SPARE_ROW + 4 * q : SPARE_ROW + 4 * q + 4, :].bitcast(I32))
        nc.sync.dma_start(out=gv_sb[:], in_=gv.rearrange("(p t) -> p t", t=PACK))
        load_page(1)
        load_weight("w3", w3, 0)
        load_weight("w3", w3, 1)
        load_page(2)
        load_page(3)
        nc.sync.dma_start(idx3[:], offs3)
        load_weight("w4", w4, 0)
        nc.sync.dma_start(out=w5_in[:], in_=w5_words[0].rearrange("p c i -> p (c i)").bitcast(I32))
        for q in range(QUADS):
            nc.sync.dma_start(out=w5_plane_in[plane_rows(q), :].bitcast(I32),
                              in_=w5_scales[0, scale_rows(q), :].bitcast(I32))

        quantise_weight("w1", 1, DEALT_AT[1])
        for t in range(2):
            fetch_old(t)
            larger_reading(t)
        quantise_weight("w3", 0, DEALT_AT[0])
        quantise_weight("w3", 1, DEALT_AT[1], parts=2)
        for t in range(2, PACK):
            fetch_old(t)

        for t in range(PACK):
            h = kept([P, S], F32, "h")
            for half in range(S // BANK):
                cols = slice(half * BANK, (half + 1) * BANK)
                d_ps = bank([P, BANK], "d%d_%d" % (t, half), D_BANK + half)
                first_product(d_ps, "w3", t, cols)
                th = work.tile([P, BANK], F32, name="th")
                nc.scalar.activation(th[:], d_ps[:], ACT.Tanh)
                bounded = work.tile([P, BANK], F32, name="bounded")
                nc.scalar.activation(bounded[:], th[:], ACT.Copy, scale=gv_sb[:, t : t + 1])
                nc.gpsimd.tensor_tensor(h[:, cols], larger[t, half][:], bounded[:], ALU.add)
            new = placed([P, S], F32, "new%d" % t, NEW_AT[t % 2])
            nc.vector.tensor_tensor(new[:], h[:], old[t][:], ALU.max)
            if t + 2 < PACK:
                larger_reading(t + 2)
            nc.vector.tensor_copy(page[t][:].indirect(idx2[:]), new[:])
            if t == 1:
                quantise_weight("w4", 0, DEALT_AT[0])
                w5_codes = kept([P, N], I32, "w5_codes")
                nc.gpsimd.tensor_copy(w5_codes[:].rearrange("p (t m) -> p m t", t=PACK),
                                      w5_in[:].rearrange("p (m t) -> p m t", t=PACK))
                w5_plane = kept([P, N], U8, "w5_plane")
                nc.gpsimd.tensor_copy(w5_plane[:].rearrange("p (t m) -> p t m", t=PACK),
                                      w5_plane_in[:].rearrange("p (m t) -> p t m", t=PACK))

        y_codes = kept([P, M], I32, "y_codes")
        y_plane = kept([P, M], U8, "y_plane")
        out_rows = out_0.rearrange("(p t) m -> p t m", t=PACK)
        out_words = out_1[0].rearrange("p m i -> p (m i)").bitcast(I32)
        per_bank = BANK // CHUNK
        x_bf, x_codes, x_plane, e_ps, gate, y_bf = {}, {}, {}, {}, {}, {}

        def interleave(copy, dst, src):
            copy(dst[:].rearrange("p (g i t) -> p g t i", i=RUN, t=PACK),
                 src[:].rearrange("p t (g i) -> p g t i", i=RUN))

        def look_up(c):
            picked = placed([P, PACK, CHUNK], BF16, "picked%d" % c, PICKED_AT[c])
            entries = idx3[:, c * CHUNK // 16 : (c + 1) * CHUNK // 16]
            for t in range(PACK):
                nc.vector.tensor_copy(picked[:, t, :], page[t][:].indirect(entries))
            x_bf[c] = placed([P, PACK * CHUNK], BF16, "x_bf%d" % c, X_BF_AT[c])
            interleave(nc.scalar.copy, x_bf[c], picked)

        def quantise_x(c):
            x_codes[c] = placed([P, CHUNK], U32, "x_codes%d" % c, X_CODES_AT[c])
            x_plane[c] = kept([P, CHUNK], U8, "x_plane%d" % c)
            nc.vector.quantize_mx(out=x_codes[c][:].bitcast(FP8X4), scales=x_plane[c][:], in_=x_bf[c][:])

        def products(c):
            for b in range(PACK // per_bank):
                f_ps = bank([P, per_bank, CHUNK], "f%d_%d" % (c, b), F_BANK[c % 2] + b)
                e_ps[c, b] = bank([P, per_bank, CHUNK], "e%d_%d" % (c, b), E_BANK[c % 2] + b)
                for ps, words, plane in ((f_ps, w5_codes, w5_plane), (e_ps[c, b], codes["w4", 0], planes["w4", 0])):
                    for i in range(per_bank):
                        rows = slice((b * per_bank + i) * P, (b * per_bank + i + 1) * P)
                        nc.tensor.matmul_mx(out=ps[:, i, :], lhsT=words[:, rows].bitcast(FP8X4),
                                            lhsT_scale=plane[:, rows], rhs=x_codes[c][:].bitcast(FP8X4),
                                            rhs_scale=x_plane[c][:], start=True, stop=True)
                gate[c, b] = placed([P, per_bank, CHUNK], F32, "gate%d_%d" % (c, b), GATE_AT[c % 2] + 2 * b)
                nc.scalar.activation(gate[c, b][:], f_ps[:], ACT.Sigmoid)

        def results(c):
            y = kept([P, PACK, CHUNK], F32, "y%d" % c)
            for b in range(PACK // per_bank):
                nc.vector.tensor_tensor(y[:, b * per_bank : (b + 1) * per_bank, :], e_ps[c, b][:], gate[c, b][:],
                                        ALU.add)
            nc.sync.dma_start(out=out_rows[:, :, c * CHUNK : (c + 1) * CHUNK], in_=y[:])
            y_bf[c] = kept([P, PACK * CHUNK], BF16, "y_bf%d" % c)
            interleave(nc.vector.tensor_copy if c == CHUNKS - 1 else nc.scalar.copy, y_bf[c], y)

        def quantise_y(c):
            cols = slice(c * CHUNK, (c + 1) * CHUNK)
            nc.vector.quantize_mx(out=y_codes[:, cols].bitcast(FP8X4), scales=y_plane[:, cols], in_=y_bf[c][:])
            nc.sync.dma_start(out=out_words[:, cols], in_=y_codes[:, cols])

        pipeline = ((results, 3), (look_up, 0), (quantise_x, 1), (products, 1), (quantise_y, 4))
        for i in range(CHUNKS + 4):
            for step, lag in pipeline:
                if 0 <= i - lag < CHUNKS:
                    step(i - lag)
        for q in range(QUADS):
            (nc.sync, nc.scalar)[q % 2].dma_start(out=out_2[0, scale_rows(q), :].bitcast(I32),
                                                  in_=y_plane[plane_rows(q), :].bitcast(I32))
